import numpy as np
import ml_dtypes


def mxq(x, axis, fmt="e4m3"):
    dtype, down = {"e4m3": (ml_dtypes.float8_e4m3fn, 7), "e5m2": (ml_dtypes.float8_e5m2, 14)}[fmt]
    v = np.moveaxis(np.asarray(x, np.float32).astype(ml_dtypes.bfloat16).astype(np.float64), axis, -1)
    blocks = v.reshape(v.shape[:-1] + (-1, 32))
    amax = np.abs(blocks).max(-1, keepdims=True)
    byte = np.maximum(np.where(amax > 0, np.frexp(amax)[1] - 1 + 127, 0) - down, 1)
    scale = np.exp2(byte - 127.0)
    codes = (blocks / scale).astype(np.float32).astype(dtype).astype(np.float64)
    return np.moveaxis((codes * scale).reshape(v.shape), -1, axis)


WIDE = False


def mx_kscale(k):
    if not WIDE:
        return np.ones(k)
    levels = np.array([30, -30])
    if k % 512:
        return np.exp2(np.random.permutation(np.resize(levels, k // 32))).repeat(32)
    a = np.empty((k // 512, 16))
    for p in range(k // 512):
        a[p, :8] = np.random.permutation(np.resize(levels, 8))
        for g in range(8):
            far = levels[np.abs(levels - a[p, g]) >= 10]
            a[p, g + 8] = far[np.random.randint(len(far))]
    return np.exp2(a.ravel()).repeat(32)


def f64(x):
    return np.asarray(x).astype(np.float64)


def striped(idx):
    return np.tile(np.asarray(idx).reshape(-1, 16).T, (8, 1)).astype(np.uint16)


def unstriped(offs):
    return offs[:16].T.reshape(-1).astype(np.int64)


def bf(x):
    return np.asarray(x, np.float32).astype(ml_dtypes.bfloat16)


def planes(Y):
    r, m = Y.shape
    b = f64(bf(Y)).reshape(r // 32, 32, m)
    amax = np.abs(b).max(1)
    byte = np.clip(np.where(amax > 0, np.frexp(amax)[1] - 1 + 127 - 7, 1), 1, 254)
    codes = (b * np.exp2(127.0 - byte)[:, None, :]).reshape(r, m).astype(np.float32).astype(ml_dtypes.float8_e4m3fn).view(np.uint8)
    words = codes.reshape(r // 512, 128, 4, m).transpose(0, 1, 3, 2)
    return np.ascontiguousarray(words), np.ascontiguousarray(byte.astype(np.uint8).reshape(r // 512, 16, m))


K, J, N, T, V = 512, 512, 256, 1024, 1024


def setup_inputs():
    n = np.random.standard_normal
    idx = np.random.permutation(T)[:J]
    idx2 = np.random.permutation(V)[:J]
    fj = mx_kscale(J)
    return {
        "xf": (n((K, T))).astype(np.float32),
        "ra": (np.random.uniform(0.5, 1.5, (1, J)) * fj).astype(np.float32),
        "ow": (n((K, J)) * 0.7).astype(np.float32),
        "gt": (n((N, V)) * np.exp(0.5 * n((1, V)))).astype(np.float32),
        "rb": (np.random.uniform(0.5, 1.5, (1, J)) / fj).astype(np.float32),
        "pr": (n((N, J))).astype(np.float32),
        "old": (1.0 * n((K, N))).astype(np.float32),
        "offs": striped(idx),
        "offs2": striped(idx2),
    }


def reference(xf, ra, ow, gt, rb, pr, old, offs, offs2):
    idx = unstriped(offs)
    idx2 = unstriped(offs2)
    us = (f64(xf)[:, idx] - f64(ow)) * f64(ra)
    uj = us.T
    gs = (f64(gt)[:, idx2] - f64(pr)) * f64(rb)
    gj = gs.T
    ujq = mxq(uj, 0, "e5m2")
    gjq = mxq(gj, 0, "e5m2")
    w = ujq.T @ gjq
    pk1 = np.max(np.abs(w), axis=1, keepdims=True)
    y = w / (pk1 + 2.0) - 0.3 * f64(old)
    words, scales = planes(y)
    return y, words, scales

@@ -1,0 +1,155 @@
+from contextlib import ExitStack
+
+import concourse.mybir as mybir
+from concourse.masks import make_identity
+
+K, J, N, T = 512, 512, 256, 1024
+FLOPS = 2 * K * J * N
+
+F32 = mybir.dt.float32
+BF16 = mybir.dt.bfloat16
+I32 = mybir.dt.int32
+U32 = mybir.dt.uint32
+U16 = mybir.dt.uint16
+U8 = mybir.dt.uint8
+E5M2X4 = mybir.dt.float8_e5m2_x4
+E4M3X4 = mybir.dt.float8_e4m3fn_x4
+ALU = mybir.AluOpType
+ACT = mybir.ActivationFunctionType
+
+P = 128
+PACK = 4
+G_BLOCKS = N // P
+TURN_BANKS = 4
+
+
+def tile_list_moment_offset_errors_rowpeaks_pl_kernel(tc, xf, ra, ow, gt, rb, pr, old, offs, offs2, out_0, out_1, out_2):
+    nc = tc.nc
+    with ExitStack() as ctx:
+        keep = ctx.enter_context(tc.tile_pool(name="keep", bufs=1))
+        psum = ctx.enter_context(tc.psum_pool(name="psum", bufs=1))
+
+        x_list = keep.tile([P, J // 16], U16, name="x_list")
+        g_list = keep.tile([P, J // 16], U16, name="g_list")
+        x_weight = keep.tile([P, PACK], F32, name="x_weight")
+        g_weight = keep.tile([P, PACK], F32, name="g_weight")
+        ident = keep.tile([P, P], F32, name="ident")
+        make_identity(nc, ident[:])
+
+        xf_rows = xf.rearrange("(p s) c -> p s c", s=PACK)
+        ow_rows = ow.rearrange("(p s) c -> p s c", s=PACK)
+        table_src = [gt[h * P : (h + 1) * P, :] for h in range(G_BLOCKS)] + [xf_rows[:, s, :] for s in range(PACK)]
+        own_src = [pr[h * P : (h + 1) * P, :] for h in range(G_BLOCKS)] + [ow_rows[:, s, :] for s in range(PACK)]
+        blocks = G_BLOCKS + PACK
+        table = [keep.tile([P, T], F32, name="table%d" % b) for b in range(blocks)]
+        own = [keep.tile([P, J], F32, name="own%d" % b) for b in range(blocks)]
+        old_sb = keep.tile([P, PACK, N], F32, name="old_sb")
+
+        nc.scalar.dma_start(out=g_weight[:], in_=rb.rearrange("o (p t) -> (o p) t", t=PACK))
+        nc.scalar.dma_start(out=x_weight[:], in_=ra.rearrange("o (p t) -> (o p) t", t=PACK))
+        for b in range(blocks):
+            nc.sync.dma_start(out=own[b][:], in_=own_src[b])
+            if b == 0:
+                nc.sync.dma_start(g_list[:], offs2)
+            if b == G_BLOCKS:
+                nc.sync.dma_start(x_list[:], offs)
+            nc.sync.dma_start(out=table[b][:], in_=table_src[b])
+        nc.sync.dma_start(out=old_sb[:], in_=old.rearrange("(p s) n -> p s n", s=PACK))
+
+        g_codes = keep.tile([P, N], U32, name="g_codes", align_bytes=64)
+        g_scales = keep.tile([P, N], U8, name="g_scales", align_bytes=64)
+        u_codes = [keep.tile([P, P], U32, name="u_codes%d" % s, align_bytes=64) for s in range(PACK)]
+        u_scales = [keep.tile([P, P], U8, name="u_scales%d" % s, align_bytes=64) for s in range(PACK)]
+        moment = [psum.tile([P, N], F32, name="moment%d" % s) for s in range(PACK)]
+        magnitude = [keep.tile([P, N], F32, name="magnitude%d" % s) for s in range(PACK)]
+        denom = [keep.tile([P, 1], F32, name="denom%d" % s) for s in range(PACK)]
+        recip = [keep.tile([P, 1], F32, name="recip%d" % s) for s in range(PACK)]
+        decay = keep.tile([P, PACK, N], F32, name="decay")
+        y = keep.tile([P, PACK, N], F32, name="y")
+        y_grouped = keep.tile([P, N, PACK], BF16, name="y_grouped", align_bytes=64)
+        y_codes = keep.tile([P, N], U32, name="y_codes", align_bytes=64)
+        y_scales = keep.tile([P, N], U8, name="y_scales", align_bytes=64)
+        out_rows = out_0.rearrange("(p s) n -> p s n", s=PACK)
+
+        def turn(b):
+            slots = g_list if b < G_BLOCKS else x_list
+            bank = psum.tile([P, PACK, P], F32, name="turn%d" % b, tag="turn%d" % (b % TURN_BANKS))
+            dealt = keep.tile([P, PACK, P], F32, name="dealt%d" % b)
+            nc.vector.tensor_scalar(
+                out=dealt[:].rearrange("p t m -> p m t"),
+                in0=own[b][:].rearrange("p (m t) -> p m t", t=PACK),
+                scalar1=-1.0, scalar2=None, op0=ALU.mult,
+            )
+            for t in range(PACK):
+                nc.tensor.matmul(bank[:, t, :], lhsT=dealt[:, t, :], rhs=ident[:], is_transpose=True, start=(t == 0), stop=False)
+            picked = keep.tile([P, J], F32, name="picked%d" % b)
+            if b == blocks - 1:
+                half = J // 2
+                nc.scalar.activation(picked[:, :half], table[b][:].indirect(slots[:, : half // 16]), ACT.Copy)
+                nc.vector.tensor_copy(picked[:, half:], table[b][:].indirect(slots[:, half // 16 :]))
+            else:
+                nc.scalar.activation(picked[:], table[b][:].indirect(slots[:]), ACT.Copy)
+            for t in range(PACK):
+                nc.tensor.matmul(bank[:, t, :], lhsT=picked[:, t::PACK], rhs=ident[:], is_transpose=True, start=False, stop=(t == PACK - 1))
+            return bank
+
+        def quantise(b, bank):
+            weight = g_weight if b < G_BLOCKS else x_weight
+            grouped = keep.tile([P, P, PACK], BF16, name="grouped%d" % b, align_bytes=64)
+            nc.vector.tensor_tensor(
+                out=grouped[:],
+                in0=bank[:].rearrange("p t c -> p c t"),
+                in1=weight[:].unsqueeze(1).to_broadcast([P, P, PACK]),
+                op=ALU.mult,
+            )
+            if b < G_BLOCKS:
+                codes, scales = g_codes[:, b * P : (b + 1) * P], g_scales[:, b * P : (b + 1) * P]
+            else:
+                codes, scales = u_codes[b - G_BLOCKS][:], u_scales[b - G_BLOCKS][:]
+            nc.vector.quantize_mx(out=codes.bitcast(E5M2X4), scales=scales, in_=grouped[:].rearrange("p c t -> p (c t)"))
+
+        def multiply(s):
+            nc.tensor.matmul_mx(
+                out=moment[s][:],
+                lhsT=u_codes[s][:].bitcast(E5M2X4), lhsT_scale=u_scales[s][:],
+                rhs=g_codes[:].bitcast(E5M2X4), rhs_scale=g_scales[:],
+                start=True, stop=True,
+            )
+            nc.scalar.activation(magnitude[s][:], moment[s][:], ACT.Abs)
+            nc.vector.tensor_scalar(
+                out=magnitude[s][:], in0=magnitude[s][:], scalar1=2.0, scalar2=None,
+                op0=ALU.add, op1=ALU.max, accum_out=denom[s][:],
+            )
+            nc.vector.reciprocal(recip[s][:], denom[s][:])
+
+        def finish(s):
+            nc.vector.scalar_tensor_tensor(
+                out=y[:, s, :], in0=moment[s][:], scalar=recip[s][:], in1=decay[:, s, :], op0=ALU.mult, op1=ALU.add,
+            )
+            nc.sync.dma_start(out=out_rows[:, s, :], in_=y[:, s, :])
+
+        def group_pair(first):
+            nc.vector.tensor_copy(
+                out=y_grouped[:, :, first : first + 2],
+                in_=y[:, first : first + 2, :].rearrange("p s n -> p n s"),
+            )
+
+        for b in range(blocks):
+            bank = turn(b)
+            if b > G_BLOCKS:
+                multiply(b - 1 - G_BLOCKS)
+            quantise(b, bank)
+        for s in range(PACK):
+            nc.scalar.activation(decay[:, s, :], old_sb[:, s, :], ACT.Copy, scale=-0.3)
+        for s in range(PACK - 1):
+            finish(s)
+        group_pair(0)
+        multiply(PACK - 1)
+        finish(PACK - 1)
+        group_pair(2)
+        nc.vector.quantize_mx(out=y_codes[:].bitcast(E4M3X4), scales=y_scales[:], in_=y_grouped[:].rearrange("p n s -> p (n s)"))
+        nc.sync.dma_start(out=out_1.rearrange("z l c r -> (z l) (c r)").bitcast(I32), in_=y_codes[:].bitcast(I32))
+        scale_rows = out_2.rearrange("z q c -> (z q) c").bitcast(I32)
+        for q in range(4):
+            queue = nc.sync if q % 2 else nc.scalar
+            queue.dma_start(out=scale_rows[4 * q : 4 * q + 4, :], in_=y_scales[32 * q : 32 * q + 4, :].bitcast(I32))

@@ -35,6 +35,9 @@ def tile_list_moment_offset_errors_rowpeaks_pl_kernel(tc, xf, ra, ow, gt, rb, pr
         g_weight = keep.tile([P, PACK], F32, name="g_weight")
         ident = keep.tile([P, P], F32, name="ident")
         make_identity(nc, ident[:])
+        warm = keep.tile([P, 1], F32, name="warm")
+        nc.vector.memset(warm[:], 0.0)
+        nc.scalar.activation(warm[:], warm[:], ACT.Abs)
 
         xf_rows = xf.rearrange("(p s) c -> p s c", s=PACK)
         ow_rows = ow.rearrange("(p s) c -> p s c", s=PACK)
@@ -42,18 +45,20 @@ def tile_list_moment_offset_errors_rowpeaks_pl_kernel(tc, xf, ra, ow, gt, rb, pr
         own_src = [pr[h * P : (h + 1) * P, :] for h in range(G_BLOCKS)] + [ow_rows[:, s, :] for s in range(PACK)]
         blocks = G_BLOCKS + PACK
         table = [keep.tile([P, T], F32, name="table%d" % b) for b in range(blocks)]
-        own = [keep.tile([P, J], F32, name="own%d" % b) for b in range(blocks)]
+        own = [keep.tile([P, J], F32, name="own%d" % b, align_bytes=64) for b in range(blocks)]
         old_sb = keep.tile([P, PACK, N], F32, name="old_sb")
 
-        nc.scalar.dma_start(out=g_weight[:], in_=rb.rearrange("o (p t) -> (o p) t", t=PACK))
-        nc.scalar.dma_start(out=x_weight[:], in_=ra.rearrange("o (p t) -> (o p) t", t=PACK))
         for b in range(blocks):
-            nc.sync.dma_start(out=own[b][:], in_=own_src[b])
+            nc.sync.dma_start(out=table[b][:], in_=table_src[b])
             if b == 0:
                 nc.sync.dma_start(g_list[:], offs2)
-            if b == G_BLOCKS:
+            nc.sync.dma_start(out=own[b][:], in_=own_src[b])
+            if b == 0:
+                nc.sync.dma_start(out=g_weight[:], in_=rb.rearrange("o (p t) -> (o p) t", t=PACK))
+            if b == G_BLOCKS - 1:
                 nc.sync.dma_start(x_list[:], offs)
-            nc.sync.dma_start(out=table[b][:], in_=table_src[b])
+            if b == G_BLOCKS:
+                nc.sync.dma_start(out=x_weight[:], in_=ra.rearrange("o (p t) -> (o p) t", t=PACK))
         nc.sync.dma_start(out=old_sb[:], in_=old.rearrange("(p s) n -> p s n", s=PACK))
 
         g_codes = keep.tile([P, N], U32, name="g_codes", align_bytes=64)
@@ -61,10 +66,9 @@ def tile_list_moment_offset_errors_rowpeaks_pl_kernel(tc, xf, ra, ow, gt, rb, pr
         u_codes = [keep.tile([P, P], U32, name="u_codes%d" % s, align_bytes=64) for s in range(PACK)]
         u_scales = [keep.tile([P, P], U8, name="u_scales%d" % s, align_bytes=64) for s in range(PACK)]
         moment = [psum.tile([P, N], F32, name="moment%d" % s) for s in range(PACK)]
-        magnitude = [keep.tile([P, N], F32, name="magnitude%d" % s) for s in range(PACK)]
         denom = [keep.tile([P, 1], F32, name="denom%d" % s) for s in range(PACK)]
         recip = [keep.tile([P, 1], F32, name="recip%d" % s) for s in range(PACK)]
-        decay = keep.tile([P, PACK, N], F32, name="decay")
+        decay = [keep.tile([P, 2, N], F32, name="decay%d" % h, align_bytes=64) for h in range(2)]
         y = keep.tile([P, PACK, N], F32, name="y")
         y_grouped = keep.tile([P, N, PACK], BF16, name="y_grouped", align_bytes=64)
         y_codes = keep.tile([P, N], U32, name="y_codes", align_bytes=64)
@@ -74,6 +78,8 @@ def tile_list_moment_offset_errors_rowpeaks_pl_kernel(tc, xf, ra, ow, gt, rb, pr
         def turn(b):
             slots = g_list if b < G_BLOCKS else x_list
             bank = psum.tile([P, PACK, P], F32, name="turn%d" % b, tag="turn%d" % (b % TURN_BANKS))
+            picked = keep.tile([P, J], F32, name="picked%d" % b)
+            nc.scalar.activation(picked[:], table[b][:].indirect(slots[:]), ACT.Copy)
             dealt = keep.tile([P, PACK, P], F32, name="dealt%d" % b)
             nc.vector.tensor_scalar(
                 out=dealt[:].rearrange("p t m -> p m t"),
@@ -82,26 +88,23 @@ def tile_list_moment_offset_errors_rowpeaks_pl_kernel(tc, xf, ra, ow, gt, rb, pr
             )
             for t in range(PACK):
                 nc.tensor.matmul(bank[:, t, :], lhsT=dealt[:, t, :], rhs=ident[:], is_transpose=True, start=(t == 0), stop=False)
-            picked = keep.tile([P, J], F32, name="picked%d" % b)
-            if b == blocks - 1:
-                half = J // 2
-                nc.scalar.activation(picked[:, :half], table[b][:].indirect(slots[:, : half // 16]), ACT.Copy)
-                nc.vector.tensor_copy(picked[:, half:], table[b][:].indirect(slots[:, half // 16 :]))
-            else:
-                nc.scalar.activation(picked[:], table[b][:].indirect(slots[:]), ACT.Copy)
             for t in range(PACK):
                 nc.tensor.matmul(bank[:, t, :], lhsT=picked[:, t::PACK], rhs=ident[:], is_transpose=True, start=False, stop=(t == PACK - 1))
             return bank
 
-        def quantise(b, bank):
+        def weigh(b, bank):
             weight = g_weight if b < G_BLOCKS else x_weight
-            grouped = keep.tile([P, P, PACK], BF16, name="grouped%d" % b, align_bytes=64)
+            grouped = keep.tile([P, P, PACK], BF16, name="grouped%d" % b, align_bytes=64,
+                                tag=("own%d" % (b + 1) if b + 1 < blocks else "grouped_last"))
             nc.vector.tensor_tensor(
                 out=grouped[:],
                 in0=bank[:].rearrange("p t c -> p c t"),
                 in1=weight[:].unsqueeze(1).to_broadcast([P, P, PACK]),
                 op=ALU.mult,
             )
+            return grouped
+
+        def quantise(b, grouped):
             if b < G_BLOCKS:
                 codes, scales = g_codes[:, b * P : (b + 1) * P], g_scales[:, b * P : (b + 1) * P]
             else:
@@ -115,39 +118,63 @@ def tile_list_moment_offset_errors_rowpeaks_pl_kernel(tc, xf, ra, ow, gt, rb, pr
                 rhs=g_codes[:].bitcast(E5M2X4), rhs_scale=g_scales[:],
                 start=True, stop=True,
             )
-            nc.scalar.activation(magnitude[s][:], moment[s][:], ACT.Abs)
+
+        def peak(s):
+            magnitude = keep.tile([P, N], F32, name="magnitude%d" % s, tag=("table%d" % (blocks - 1) if s == 0 else "magnitude%d" % s))
+            nc.scalar.activation(magnitude[:], moment[s][:], ACT.Abs)
             nc.vector.tensor_scalar(
-                out=magnitude[s][:], in0=magnitude[s][:], scalar1=2.0, scalar2=None,
+                out=magnitude[:], in0=magnitude[:], scalar1=2.0, scalar2=None,
                 op0=ALU.add, op1=ALU.max, accum_out=denom[s][:],
             )
+
+        def invert(s):
             nc.vector.reciprocal(recip[s][:], denom[s][:])
 
-        def finish(s):
+        def finish(s, cols=slice(0, N)):
             nc.vector.scalar_tensor_tensor(
-                out=y[:, s, :], in0=moment[s][:], scalar=recip[s][:], in1=decay[:, s, :], op0=ALU.mult, op1=ALU.add,
-            )
-            nc.sync.dma_start(out=out_rows[:, s, :], in_=y[:, s, :])
-
-        def group_pair(first):
-            nc.vector.tensor_copy(
-                out=y_grouped[:, :, first : first + 2],
-                in_=y[:, first : first + 2, :].rearrange("p s n -> p n s"),
+                out=y[:, s, cols], in0=moment[s][:, cols], scalar=recip[s][:], in1=decay[s // 2][:, s % 2, cols], op0=ALU.mult, op1=ALU.add,
             )
 
-        for b in range(blocks):
-            bank = turn(b)
+        def store(first, last):
+            nc.sync.dma_start(out=out_rows[:, first:last, :], in_=y[:, first:last, :])
+
+        banks = [turn(0)]
+        for b in range(1, blocks - 1):
+            banks.append(turn(b))
+            quantise(b - 1, weigh(b - 1, banks[b - 1]))
             if b > G_BLOCKS:
                 multiply(b - 1 - G_BLOCKS)
-            quantise(b, bank)
-        for s in range(PACK):
-            nc.scalar.activation(decay[:, s, :], old_sb[:, s, :], ACT.Copy, scale=-0.3)
-        for s in range(PACK - 1):
-            finish(s)
-        group_pair(0)
-        multiply(PACK - 1)
-        finish(PACK - 1)
-        group_pair(2)
-        nc.vector.quantize_mx(out=y_codes[:].bitcast(E4M3X4), scales=y_scales[:], in_=y_grouped[:].rearrange("p n s -> p (n s)"))
+        banks.append(turn(blocks - 1))
+        grouped = weigh(blocks - 2, banks[blocks - 2])
+        peak(0)
+        quantise(blocks - 2, grouped)
+        multiply(2)
+        invert(0)
+        peak(1)
+        invert(1)
+        for h in range(2):
+            nc.scalar.activation(decay[h][:], old_sb[:, 2 * h : 2 * h + 2, :], ACT.Copy, scale=-0.3)
+        grouped = weigh(blocks - 1, banks[blocks - 1])
+        finish(0)
+        quantise(blocks - 1, grouped)
+        multiply(3)
+        finish(1)
+        store(0, 2)
+        peak(2)
+        invert(2)
+        finish(2)
+        store(2, 3)
+        nc.scalar.copy(out=y_grouped[:, :, 0:2], in_=y[:, 0:2, :].rearrange("p s n -> p n s"))
+        peak(3)
+        invert(3)
+        halves = [slice(0, N // 2), slice(N // 2, N)]
+        for cols in halves:
+            finish(3, cols)
+        store(3, 4)
+        for cols in halves:
+            nc.vector.tensor_copy(out=y_grouped[:, cols, 2:4], in_=y[:, 2:4, cols].rearrange("p s n -> p n s"))
+        for cols in halves:
+            nc.vector.quantize_mx(out=y_codes[:, cols].bitcast(E4M3X4), scales=y_scales[:, cols], in_=y_grouped[:, cols, :].rearrange("p n s -> p (n s)"))
         nc.sync.dma_start(out=out_1.rearrange("z l c r -> (z l) (c r)").bitcast(I32), in_=y_codes[:].bitcast(I32))
         scale_rows = out_2.rearrange("z q c -> (z q) c").bitcast(I32)
         for q in range(4):

@@ -34,6 +34,8 @@ def tile_list_moment_offset_errors_rowpeaks_pl_kernel(tc, xf, ra, ow, gt, rb, pr
         x_weight = keep.tile([P, PACK], F32, name="x_weight")
         g_weight = keep.tile([P, PACK], F32, name="g_weight")
         ident = keep.tile([P, P], F32, name="ident")
+        nc.scalar.dma_start(out=g_weight[:], in_=rb.rearrange("o (p t) -> (o p) t", t=PACK))
+        nc.scalar.dma_start(out=x_weight[:], in_=ra.rearrange("o (p t) -> (o p) t", t=PACK))
         make_identity(nc, ident[:])
         warm = keep.tile([P, 1], F32, name="warm")
         nc.vector.memset(warm[:], 0.0)
@@ -53,23 +55,19 @@ def tile_list_moment_offset_errors_rowpeaks_pl_kernel(tc, xf, ra, ow, gt, rb, pr
             if b == 0:
                 nc.sync.dma_start(g_list[:], offs2)
             nc.sync.dma_start(out=own[b][:], in_=own_src[b])
-            if b == 0:
-                nc.sync.dma_start(out=g_weight[:], in_=rb.rearrange("o (p t) -> (o p) t", t=PACK))
             if b == G_BLOCKS - 1:
                 nc.sync.dma_start(x_list[:], offs)
-            if b == G_BLOCKS:
-                nc.sync.dma_start(out=x_weight[:], in_=ra.rearrange("o (p t) -> (o p) t", t=PACK))
         nc.sync.dma_start(out=old_sb[:], in_=old.rearrange("(p s) n -> p s n", s=PACK))
 
         g_codes = keep.tile([P, N], U32, name="g_codes", align_bytes=64)
         g_scales = keep.tile([P, N], U8, name="g_scales", align_bytes=64)
         u_codes = [keep.tile([P, P], U32, name="u_codes%d" % s, align_bytes=64) for s in range(PACK)]
         u_scales = [keep.tile([P, P], U8, name="u_scales%d" % s, align_bytes=64) for s in range(PACK)]
-        moment = [psum.tile([P, N], F32, name="moment%d" % s) for s in range(PACK)]
+        moment = []
         denom = [keep.tile([P, 1], F32, name="denom%d" % s) for s in range(PACK)]
         recip = [keep.tile([P, 1], F32, name="recip%d" % s) for s in range(PACK)]
         decay = [keep.tile([P, 2, N], F32, name="decay%d" % h, align_bytes=64) for h in range(2)]
-        y = keep.tile([P, PACK, N], F32, name="y")
+        y = [keep.tile([P, 2, N], F32, name="y%d" % h) for h in range(2)]
         y_grouped = keep.tile([P, N, PACK], BF16, name="y_grouped", align_bytes=64)
         y_codes = keep.tile([P, N], U32, name="y_codes", align_bytes=64)
         y_scales = keep.tile([P, N], U8, name="y_scales", align_bytes=64)
@@ -82,8 +80,8 @@ def tile_list_moment_offset_errors_rowpeaks_pl_kernel(tc, xf, ra, ow, gt, rb, pr
             nc.scalar.activation(picked[:], table[b][:].indirect(slots[:]), ACT.Copy)
             dealt = keep.tile([P, PACK, P], F32, name="dealt%d" % b)
             nc.vector.tensor_scalar(
-                out=dealt[:].rearrange("p t m -> p m t"),
-                in0=own[b][:].rearrange("p (m t) -> p m t", t=PACK),
+                out=dealt[:].rearrange("p t (c i) -> p c t i", i=PACK),
+                in0=own[b][:].rearrange("p (c i t) -> p c t i", i=PACK, t=PACK),
                 scalar1=-1.0, scalar2=None, op0=ALU.mult,
             )
             for t in range(PACK):
@@ -112,6 +110,8 @@ def tile_list_moment_offset_errors_rowpeaks_pl_kernel(tc, xf, ra, ow, gt, rb, pr
             nc.vector.quantize_mx(out=codes.bitcast(E5M2X4), scales=scales, in_=grouped[:].rearrange("p c t -> p (c t)"))
 
         def multiply(s):
+            tag = "turn%d" % ((blocks - 2) % TURN_BANKS) if s == 1 else "moment%d" % s
+            moment.append(psum.tile([P, N], F32, name="moment%d" % s, tag=tag))
             nc.tensor.matmul_mx(
                 out=moment[s][:],
                 lhsT=u_codes[s][:].bitcast(E5M2X4), lhsT_scale=u_scales[s][:],
@@ -132,47 +132,47 @@ def tile_list_moment_offset_errors_rowpeaks_pl_kernel(tc, xf, ra, ow, gt, rb, pr
 
         def finish(s, cols=slice(0, N)):
             nc.vector.scalar_tensor_tensor(
-                out=y[:, s, cols], in0=moment[s][:, cols], scalar=recip[s][:], in1=decay[s // 2][:, s % 2, cols], op0=ALU.mult, op1=ALU.add,
+                out=y[s // 2][:, s % 2, cols], in0=moment[s][:, cols], scalar=recip[s][:], in1=decay[s // 2][:, s % 2, cols], op0=ALU.mult, op1=ALU.add,
             )
 
-        def store(first, last):
-            nc.sync.dma_start(out=out_rows[:, first:last, :], in_=y[:, first:last, :])
+        def store(h):
+            nc.sync.dma_start(out=out_rows[:, 2 * h : 2 * h + 2, :], in_=y[h][:])
 
         banks = [turn(0)]
         for b in range(1, blocks - 1):
             banks.append(turn(b))
             quantise(b - 1, weigh(b - 1, banks[b - 1]))
-            if b > G_BLOCKS:
-                multiply(b - 1 - G_BLOCKS)
+            if b == G_BLOCKS + 1:
+                multiply(0)
         banks.append(turn(blocks - 1))
         grouped = weigh(blocks - 2, banks[blocks - 2])
         peak(0)
         quantise(blocks - 2, grouped)
-        multiply(2)
         invert(0)
-        peak(1)
-        invert(1)
+        multiply(1)
+        multiply(2)
         for h in range(2):
             nc.scalar.activation(decay[h][:], old_sb[:, 2 * h : 2 * h + 2, :], ACT.Copy, scale=-0.3)
         grouped = weigh(blocks - 1, banks[blocks - 1])
         finish(0)
         quantise(blocks - 1, grouped)
         multiply(3)
-        finish(1)
-        store(0, 2)
+        peak(1)
         peak(2)
+        invert(1)
         invert(2)
-        finish(2)
-        store(2, 3)
-        nc.scalar.copy(out=y_grouped[:, :, 0:2], in_=y[:, 0:2, :].rearrange("p s n -> p n s"))
         peak(3)
+        finish(1)
         invert(3)
+        store(0)
+        nc.scalar.copy(out=y_grouped[:, :, 0:2], in_=y[0][:].rearrange("p s n -> p n s"))
+        finish(2)
         halves = [slice(0, N // 2), slice(N // 2, N)]
         for cols in halves:
             finish(3, cols)
-        store(3, 4)
+        store(1)
         for cols in halves:
-            nc.vector.tensor_copy(out=y_grouped[:, cols, 2:4], in_=y[:, 2:4, cols].rearrange("p s n -> p n s"))
+            nc.vector.tensor_copy(out=y_grouped[:, cols, 2:4], in_=y[1][:, :, cols].rearrange("p s n -> p n s"))
         for cols in halves:
             nc.vector.quantize_mx(out=y_codes[:, cols].bitcast(E4M3X4), scales=y_scales[:, cols], in_=y_grouped[:, cols, :].rearrange("p n s -> p (n s)"))
         nc.sync.dma_start(out=out_1.rearrange("z l c r -> (z l) (c r)").bitcast(I32), in_=y_codes[:].bitcast(I32))

from contextlib import ExitStack

import concourse.mybir as mybir
from concourse.masks import make_identity

K, J, N, T = 512, 512, 256, 1024
FLOPS = 2 * K * J * N

F32 = mybir.dt.float32
BF16 = mybir.dt.bfloat16
I32 = mybir.dt.int32
U32 = mybir.dt.uint32
U16 = mybir.dt.uint16
U8 = mybir.dt.uint8
E5M2X4 = mybir.dt.float8_e5m2_x4
E4M3X4 = mybir.dt.float8_e4m3fn_x4
ALU = mybir.AluOpType
ACT = mybir.ActivationFunctionType

P = 128
PACK = 4
G_BLOCKS = N // P
TURN_BANKS = 4


def tile_list_moment_offset_errors_rowpeaks_pl_kernel(tc, xf, ra, ow, gt, rb, pr, old, offs, offs2, out_0, out_1, out_2):
    nc = tc.nc
    with ExitStack() as ctx:
        keep = ctx.enter_context(tc.tile_pool(name="keep", bufs=1))
        psum = ctx.enter_context(tc.psum_pool(name="psum", bufs=1))

        x_list = keep.tile([P, J // 16], U16, name="x_list")
        g_list = keep.tile([P, J // 16], U16, name="g_list")
        x_weight = keep.tile([P, PACK], F32, name="x_weight")
        g_weight = keep.tile([P, PACK], F32, name="g_weight")
        ident = keep.tile([P, P], F32, name="ident")
        nc.scalar.dma_start(out=g_weight[:], in_=rb.rearrange("o (p t) -> (o p) t", t=PACK))
        nc.scalar.dma_start(out=x_weight[:], in_=ra.rearrange("o (p t) -> (o p) t", t=PACK))
        make_identity(nc, ident[:])
        warm = keep.tile([P, 1], F32, name="warm")
        nc.vector.memset(warm[:], 0.0)
        nc.scalar.activation(warm[:], warm[:], ACT.Abs)

        xf_rows = xf.rearrange("(p s) c -> p s c", s=PACK)
        ow_rows = ow.rearrange("(p s) c -> p s c", s=PACK)
        table_src = [gt[h * P : (h + 1) * P, :] for h in range(G_BLOCKS)] + [xf_rows[:, s, :] for s in range(PACK)]
        own_src = [pr[h * P : (h + 1) * P, :] for h in range(G_BLOCKS)] + [ow_rows[:, s, :] for s in range(PACK)]
        blocks = G_BLOCKS + PACK
        table = [keep.tile([P, T], F32, name="table%d" % b) for b in range(blocks)]
        own = [keep.tile([P, J], F32, name="own%d" % b, align_bytes=64) for b in range(blocks)]
        old_sb = keep.tile([P, PACK, N], F32, name="old_sb")

        for b in range(blocks):
            nc.sync.dma_start(out=table[b][:], in_=table_src[b])
            if b == 0:
                nc.sync.dma_start(g_list[:], offs2)
            nc.sync.dma_start(out=own[b][:], in_=own_src[b])
            if b == G_BLOCKS - 1:
                nc.sync.dma_start(x_list[:], offs)
        nc.sync.dma_start(out=old_sb[:], in_=old.rearrange("(p s) n -> p s n", s=PACK))

        g_codes = keep.tile([P, N], U32, name="g_codes", align_bytes=64)
        g_scales = keep.tile([P, N], U8, name="g_scales", align_bytes=64)
        u_codes = [keep.tile([P, P], U32, name="u_codes%d" % s, align_bytes=64) for s in range(PACK)]
        u_scales = [keep.tile([P, P], U8, name="u_scales%d" % s, align_bytes=64) for s in range(PACK)]
        moment = []
        denom = [keep.tile([P, 1], F32, name="denom%d" % s) for s in range(PACK)]
        recip = [keep.tile([P, 1], F32, name="recip%d" % s) for s in range(PACK)]
        decay = [keep.tile([P, 2, N], F32, name="decay%d" % h, align_bytes=64) for h in range(2)]
        y = [keep.tile([P, 2, N], F32, name="y%d" % h) for h in range(2)]
        y_grouped = keep.tile([P, N, PACK], BF16, name="y_grouped", align_bytes=64)
        y_codes = keep.tile([P, N], U32, name="y_codes", align_bytes=64)
        y_scales = keep.tile([P, N], U8, name="y_scales", align_bytes=64)
        out_rows = out_0.rearrange("(p s) n -> p s n", s=PACK)

        def turn(b):
            slots = g_list if b < G_BLOCKS else x_list
            bank = psum.tile([P, PACK, P], F32, name="turn%d" % b, tag="turn%d" % (b % TURN_BANKS))
            picked = keep.tile([P, J], F32, name="picked%d" % b)
            nc.scalar.activation(picked[:], table[b][:].indirect(slots[:]), ACT.Copy)
            dealt = keep.tile([P, PACK, P], F32, name="dealt%d" % b)
            nc.vector.tensor_scalar(
                out=dealt[:].rearrange("p t (c i) -> p c t i", i=PACK),
                in0=own[b][:].rearrange("p (c i t) -> p c t i", i=PACK, t=PACK),
                scalar1=-1.0, scalar2=None, op0=ALU.mult,
            )
            for t in range(PACK):
                nc.tensor.matmul(bank[:, t, :], lhsT=dealt[:, t, :], rhs=ident[:], is_transpose=True, start=(t == 0), stop=False)
            for t in range(PACK):
                nc.tensor.matmul(bank[:, t, :], lhsT=picked[:, t::PACK], rhs=ident[:], is_transpose=True, start=False, stop=(t == PACK - 1))
            return bank

        def weigh(b, bank):
            weight = g_weight if b < G_BLOCKS else x_weight
            grouped = keep.tile([P, P, PACK], BF16, name="grouped%d" % b, align_bytes=64,
                                tag=("own%d" % (b + 1) if b + 1 < blocks else "grouped_last"))
            nc.vector.tensor_tensor(
                out=grouped[:],
                in0=bank[:].rearrange("p t c -> p c t"),
                in1=weight[:].unsqueeze(1).to_broadcast([P, P, PACK]),
                op=ALU.mult,
            )
            return grouped

        def quantise(b, grouped):
            if b < G_BLOCKS:
                codes, scales = g_codes[:, b * P : (b + 1) * P], g_scales[:, b * P : (b + 1) * P]
            else:
                codes, scales = u_codes[b - G_BLOCKS][:], u_scales[b - G_BLOCKS][:]
            nc.vector.quantize_mx(out=codes.bitcast(E5M2X4), scales=scales, in_=grouped[:].rearrange("p c t -> p (c t)"))

        def multiply(s):
            tag = "turn%d" % ((blocks - 2) % TURN_BANKS) if s == 1 else "moment%d" % s
            moment.append(psum.tile([P, N], F32, name="moment%d" % s, tag=tag))
            nc.tensor.matmul_mx(
                out=moment[s][:],
                lhsT=u_codes[s][:].bitcast(E5M2X4), lhsT_scale=u_scales[s][:],
                rhs=g_codes[:].bitcast(E5M2X4), rhs_scale=g_scales[:],
                start=True, stop=True,
            )

        def peak(s):
            magnitude = keep.tile([P, N], F32, name="magnitude%d" % s, tag=("table%d" % (blocks - 1) if s == 0 else "magnitude%d" % s))
            nc.scalar.activation(magnitude[:], moment[s][:], ACT.Abs)
            nc.vector.tensor_scalar(
                out=magnitude[:], in0=magnitude[:], scalar1=2.0, scalar2=None,
                op0=ALU.add, op1=ALU.max, accum_out=denom[s][:],
            )

        def invert(s):
            nc.vector.reciprocal(recip[s][:], denom[s][:])

        def finish(s, cols=slice(0, N)):
            nc.vector.scalar_tensor_tensor(
                out=y[s // 2][:, s % 2, cols], in0=moment[s][:, cols], scalar=recip[s][:], in1=decay[s // 2][:, s % 2, cols], op0=ALU.mult, op1=ALU.add,
            )

        def store(h):
            nc.sync.dma_start(out=out_rows[:, 2 * h : 2 * h + 2, :], in_=y[h][:])

        banks = [turn(0)]
        for b in range(1, blocks - 1):
            banks.append(turn(b))
            quantise(b - 1, weigh(b - 1, banks[b - 1]))
            if b == G_BLOCKS + 1:
                multiply(0)
        banks.append(turn(blocks - 1))
        grouped = weigh(blocks - 2, banks[blocks - 2])
        peak(0)
        quantise(blocks - 2, grouped)
        invert(0)
        multiply(1)
        multiply(2)
        for h in range(2):
            nc.scalar.activation(decay[h][:], old_sb[:, 2 * h : 2 * h + 2, :], ACT.Copy, scale=-0.3)
        grouped = weigh(blocks - 1, banks[blocks - 1])
        finish(0)
        quantise(blocks - 1, grouped)
        multiply(3)
        peak(1)
        peak(2)
        invert(1)
        invert(2)
        peak(3)
        finish(1)
        invert(3)
        store(0)
        nc.scalar.copy(out=y_grouped[:, :, 0:2], in_=y[0][:].rearrange("p s n -> p n s"))
        finish(2)
        halves = [slice(0, N // 2), slice(N // 2, N)]
        for cols in halves:
            finish(3, cols)
        store(1)
        for cols in halves:
            nc.vector.tensor_copy(out=y_grouped[:, cols, 2:4], in_=y[1][:, :, cols].rearrange("p s n -> p n s"))
        for cols in halves:
            nc.vector.quantize_mx(out=y_codes[:, cols].bitcast(E4M3X4), scales=y_scales[:, cols], in_=y_grouped[:, cols, :].rearrange("p n s -> p (n s)"))
        nc.sync.dma_start(out=out_1.rearrange("z l c r -> (z l) (c r)").bitcast(I32), in_=y_codes[:].bitcast(I32))
        scale_rows = out_2.rearrange("z q c -> (z q) c").bitcast(I32)
        for q in range(4):
            queue = nc.sync if q % 2 else nc.scalar
            queue.dma_start(out=scale_rows[4 * q : 4 * q + 4, :], in_=y_scales[32 * q : 32 * q + 4, :].bitcast(I32))
